import numpy as np
import ml_dtypes


def mxq(x, axis, fmt="e4m3"):
    dtype, down = {"e4m3": (ml_dtypes.float8_e4m3fn, 7), "e5m2": (ml_dtypes.float8_e5m2, 14)}[fmt]
    v = np.moveaxis(np.asarray(x, np.float32).astype(ml_dtypes.bfloat16).astype(np.float64), axis, -1)
    blocks = v.reshape(v.shape[:-1] + (-1, 32))
    amax = np.abs(blocks).max(-1, keepdims=True)
    byte = np.maximum(np.where(amax > 0, np.frexp(amax)[1] - 1 + 127, 0) - down, 1)
    scale = np.exp2(byte - 127.0)
    codes = (blocks / scale).astype(np.float32).astype(dtype).astype(np.float64)
    return np.moveaxis((codes * scale).reshape(v.shape), -1, axis)


WIDE = False


def mx_kscale(k):
    if not WIDE:
        return np.ones(k)
    levels = np.array([30, -30])
    if k % 512:
        return np.exp2(np.random.permutation(np.resize(levels, k // 32))).repeat(32)
    a = np.empty((k // 512, 16))
    for p in range(k // 512):
        a[p, :8] = np.random.permutation(np.resize(levels, 8))
        for g in range(8):
            far = levels[np.abs(levels - a[p, g]) >= 10]
            a[p, g + 8] = far[np.random.randint(len(far))]
    return np.exp2(a.ravel()).repeat(32)


def f64(x):
    return np.asarray(x).astype(np.float64)


def striped(idx):
    return np.tile(np.asarray(idx).reshape(-1, 16).T, (8, 1)).astype(np.uint16)


def unstriped(offs):
    return offs[:16].T.reshape(-1).astype(np.int64)


E2M1 = np.array([0.0, 0.5, 1.0, 1.5, 2.0, 3.0, 4.0, 6.0, -0.0, -0.5, -1.0, -1.5, -2.0, -3.0, -4.0, -6.0])


def pack_weight(w, fmt):
    k, n = w.shape
    w = f64(np.asarray(w, np.float32).astype(ml_dtypes.bfloat16)).reshape(k // 32, 32, n)
    amax = np.abs(w).max(1)
    if fmt in ("e4m3", "e5m2"):
        byte = np.frexp(amax)[1] - 1 + 127 - (7 if fmt == "e4m3" else 14)
    else:
        mant, ex = np.frexp(amax / 6.0)
        byte = np.where(mant > 0.5, ex, ex - 1) + 127
    byte = np.clip(np.where(amax > 0, byte, 1), 1, 254)
    scaled = (w * np.exp2(127.0 - byte)[:, None, :]).reshape(k, n).astype(np.float32)
    by_word = np.ascontiguousarray(scaled.reshape(k // 512, 128, 4, n).transpose(0, 1, 3, 2))
    if fmt in ("e4m3", "e5m2"):
        words = by_word.astype(ml_dtypes.float8_e4m3fn if fmt == "e4m3" else ml_dtypes.float8_e5m2).view(np.uint8)
    else:
        c = by_word.astype(ml_dtypes.float4_e2m1fn).view(np.uint8) & 0xF
        words = (c[..., 0::2] | (c[..., 1::2] << 4)).reshape(k // 512, 128, 2 * n)
    return np.ascontiguousarray(words), np.ascontiguousarray(byte.astype(np.uint8).reshape(k // 512, 16, n))


def unpack_weight(words, scales, fmt):
    g, _, n = scales.shape
    words = np.ascontiguousarray(words).reshape(g, 128, n, -1)
    if fmt in ("e4m3", "e5m2"):
        vals = words.view(ml_dtypes.float8_e4m3fn if fmt == "e4m3" else ml_dtypes.float8_e5m2).astype(np.float64)
    else:
        nib = np.empty((g, 128, n, 4), np.uint8)
        nib[..., 0::2] = words & 0xF
        nib[..., 1::2] = words >> 4
        vals = E2M1[nib]
    vals = vals * np.repeat(np.exp2(scales.astype(np.float64) - 127.0), 8, axis=1)[..., None]
    return vals.transpose(0, 1, 3, 2).reshape(g * 512, n)


K, T, J, R, O, N, S = 512, 1024, 256, 512, 128, 256, 1024


def setup_inputs():
    n = np.random.standard_normal
    idx = np.random.permutation(T)[:J]
    idx2 = np.random.permutation(J)[:O]
    idx3 = np.random.permutation(J)[:O]
    idx4 = np.random.permutation(S)[:N]
    fk = mx_kscale(K)
    fr = mx_kscale(R)
    xtp = pack_weight(n((K, T)) / fk[:, None], "e5m2")
    wp = pack_weight(n((K, R)) * 1 / np.sqrt(K) * fk[:, None], "e2m1")
    vsp = pack_weight(n((R, S)) * 1 / np.sqrt(R) / fr[:, None], "e2m1")
    return {
        "xt_words": xtp[0],
        "xt_scales": xtp[1],
        "w_words": wp[0],
        "w_scales": wp[1],
        "sa": (np.random.uniform(0.5, 1.6, (R, 1)) * fr[:, None]).astype(np.float32),
        "sb": (np.random.uniform(0.5, 1.6, (R, 1)) * fr[:, None]).astype(np.float32),
        "vs_words": vsp[0],
        "vs_scales": vsp[1],
        "offs": striped(idx),
        "offs2": striped(idx2),
        "offs3": striped(idx3),
        "offs4": striped(idx4),
    }


def reference(xt_words, xt_scales, w_words, w_scales, sa, sb, vs_words, vs_scales, offs, offs2, offs3, offs4):
    idx = unstriped(offs)
    idx2 = unstriped(offs2)
    idx3 = unstriped(offs3)
    idx4 = unstriped(offs4)
    xtu = unpack_weight(xt_words, xt_scales, "e5m2")
    wu = unpack_weight(w_words, w_scales, "e2m1")
    vsu = unpack_weight(vs_words, vs_scales, "e2m1")
    xtidxg = xtu[:, idx]
    a = wu.T @ xtidxg
    hid = np.maximum(a[:, idx2] * f64(sa), a[:, idx3] * f64(sb))
    vsidx4g = vsu[:, idx4]
    hidq = mxq(hid, 0, "e4m3")
    y = vsidx4g.T @ hidq
    return y

@@ -1,0 +1,144 @@
+from contextlib import ExitStack
+
+import concourse.mybir as mybir
+
+K, T, J, R, O, N, S = 512, 1024, 256, 512, 128, 256, 1024
+FLOPS = 2 * K * R * J + 2 * R * N * O
+
+F32 = mybir.dt.float32
+BF16 = mybir.dt.bfloat16
+I32 = mybir.dt.int32
+U32 = mybir.dt.uint32
+U16 = mybir.dt.uint16
+U8 = mybir.dt.uint8
+E5M2X4 = mybir.dt.float8_e5m2_x4
+E4M3X4 = mybir.dt.float8_e4m3fn_x4
+E2M1X4 = mybir.dt.float4_e2m1fn_x4
+COPY = mybir.ActivationFunctionType.Copy
+MAX = mybir.AluOpType.max
+
+P = 128
+PACK = 4
+QUADRANTS = 4
+QUADRANT = 32
+SCALE_ROWS = 4
+
+
+def load_scale_rows(queue, plane, scales):
+    for q in range(QUADRANTS):
+        queue.dma_start(
+            plane[QUADRANT * q : QUADRANT * q + SCALE_ROWS, :].bitcast(I32),
+            scales[0, SCALE_ROWS * q : SCALE_ROWS * (q + 1), :].bitcast(I32),
+        )
+
+
+def tile_list_weighedpicks_solo_store_plain_kernel(
+    tc, xt_words, xt_scales, w_words, w_scales, sa, sb, vs_words, vs_scales, offs, offs2, offs3, offs4, out
+):
+    nc = tc.nc
+    with ExitStack() as ctx:
+        sbuf = ctx.enter_context(tc.tile_pool(name="sbuf", bufs=1))
+        psum = ctx.enter_context(tc.psum_pool(name="psum", bufs=1))
+
+        token_list = sbuf.tile([P, J // 16], U16, name="token_list")
+        first_list = sbuf.tile([P, O // 16], U16, name="first_list")
+        second_list = sbuf.tile([P, O // 16], U16, name="second_list")
+        entry_list = sbuf.tile([P, N // 16], U16, name="entry_list")
+
+        xt_all = sbuf.tile([P, T], U32, name="xt_all", align_bytes=64)
+        xt_plane = sbuf.tile([P, T], U8, name="xt_plane", align_bytes=64)
+        w_all = sbuf.tile([P, R], U16, name="w_all", align_bytes=64)
+        w_plane = sbuf.tile([P, R], U8, name="w_plane", align_bytes=64)
+        vs_all = sbuf.tile([P, S], U16, name="vs_all", align_bytes=64)
+        vs_plane = sbuf.tile([P, S], U8, name="vs_plane", align_bytes=64)
+        first_weight = sbuf.tile([P, PACK], F32, name="first_weight")
+        second_weight = sbuf.tile([P, PACK], F32, name="second_weight")
+
+        for plane in (xt_plane, w_plane, vs_plane):
+            nc.vector.memset(plane[:].bitcast(I32), 0)
+
+        nc.sync.dma_start(token_list[:], offs)
+        nc.sync.dma_start(xt_all[:].bitcast(I32), xt_words[0].rearrange("p c b -> p (c b)").bitcast(I32))
+        nc.scalar.dma_start(w_all[:].bitcast(I32), w_words[0].bitcast(I32))
+        load_scale_rows(nc.sync, xt_plane, xt_scales)
+        load_scale_rows(nc.sync, w_plane, w_scales)
+        nc.gpsimd.dma_start(first_weight[:], sa.rearrange("(p t) o -> p (t o)", t=PACK))
+        nc.gpsimd.dma_start(second_weight[:], sb.rearrange("(p t) o -> p (t o)", t=PACK))
+        nc.sync.dma_start(first_list[:], offs2)
+        nc.sync.dma_start(second_list[:], offs3)
+        nc.sync.dma_start(entry_list[:], offs4)
+        nc.sync.dma_start(vs_all[:].bitcast(I32), vs_words[0].bitcast(I32))
+        load_scale_rows(nc.sync, vs_plane, vs_scales)
+
+        x_codes = sbuf.tile([P, J], U32, name="x_codes", align_bytes=64)
+        x_scale = sbuf.tile([P, J], U8, name="x_scale", align_bytes=64)
+        nc.vector.tensor_copy(x_scale[:], xt_plane[:].indirect(token_list[:]))
+        nc.vector.tensor_copy(x_codes[:], xt_all[:].indirect(token_list[:]))
+
+        w_scale = sbuf.tile([P, PACK, P], U8, name="w_scale", align_bytes=64)
+        nc.vector.tensor_copy(w_scale[:], w_plane[:].rearrange("p (m t) -> p t m", t=PACK))
+        w_codes = [sbuf.tile([P, P], U16, name=f"w_codes{t}", align_bytes=64) for t in range(PACK)]
+        for t in range(PACK):
+            nc.scalar.copy(w_codes[t][:], w_all[:, t::PACK])
+
+        hidden = []
+        for t in range(PACK):
+            sums = psum.tile([P, J], F32, name=f"sums{t}")
+            nc.tensor.matmul_mx(
+                out=sums[:],
+                lhsT=w_codes[t][:].bitcast(E2M1X4),
+                lhsT_scale=w_scale[:, t, :],
+                rhs=x_codes[:].bitcast(E5M2X4),
+                rhs_scale=x_scale[:],
+                start=True,
+                stop=True,
+            )
+            rows = sbuf.tile([P, J], F32, name=f"hidden{t}")
+            nc.vector.tensor_copy(rows[:], sums[:])
+            hidden.append(rows)
+
+        v_codes = sbuf.tile([P, N], U16, name="v_codes", align_bytes=64)
+        v_scale = sbuf.tile([P, N], U8, name="v_scale", align_bytes=64)
+        nc.vector.tensor_copy(v_codes[:], vs_all[:].indirect(entry_list[:]))
+        nc.vector.tensor_copy(v_scale[:], vs_plane[:].indirect(entry_list[:]))
+
+        hid = sbuf.tile([P, O, PACK], BF16, name="hid", align_bytes=64)
+        for pair in range(PACK // 2):
+            first = sbuf.tile([P, 2, O], F32, name=f"first{pair}")
+            second = sbuf.tile([P, 2, O], F32, name=f"second{pair}")
+            for i in range(2):
+                t = 2 * pair + i
+                nc.scalar.activation(
+                    first[:, i, :], hidden[t][:].indirect(first_list[:]), COPY, scale=first_weight[:, t : t + 1]
+                )
+                nc.scalar.activation(
+                    second[:, i, :], hidden[t][:].indirect(second_list[:]), COPY, scale=second_weight[:, t : t + 1]
+                )
+            nc.vector.tensor_tensor(
+                hid[:, :, 2 * pair : 2 * pair + 2],
+                first[:].rearrange("p i o -> p o i"),
+                second[:].rearrange("p i o -> p o i"),
+                MAX,
+            )
+
+        hid_codes = sbuf.tile([P, O], U32, name="hid_codes", align_bytes=64)
+        hid_scale = sbuf.tile([P, O], U8, name="hid_scale", align_bytes=64)
+        nc.vector.quantize_mx(
+            out=hid_codes[:].bitcast(E4M3X4), scales=hid_scale[:], in_=hid[:].rearrange("p o t -> p (o t)")
+        )
+
+        for half, (copy_out, queue) in enumerate(((nc.vector.tensor_copy, nc.sync), (nc.scalar.copy, nc.scalar))):
+            cols = slice(P * half, P * (half + 1))
+            product = psum.tile([P, O], F32, name=f"product{half}")
+            nc.tensor.matmul_mx(
+                out=product[:],
+                lhsT=v_codes[:, cols].bitcast(E2M1X4),
+                lhsT_scale=v_scale[:, cols],
+                rhs=hid_codes[:].bitcast(E4M3X4),
+                rhs_scale=hid_scale[:],
+                start=True,
+                stop=True,
+            )
+            result = sbuf.tile([P, O], F32, name=f"result{half}")
+            copy_out(result[:], product[:])
+            queue.dma_start(out[cols, :], result[:])

@@ -24,8 +24,8 @@ QUADRANT = 32
 SCALE_ROWS = 4
 
 
-def load_scale_rows(queue, plane, scales):
-    for q in range(QUADRANTS):
+def load_scale_rows(queue, plane, scales, quadrants):
+    for q in quadrants:
         queue.dma_start(
             plane[QUADRANT * q : QUADRANT * q + SCALE_ROWS, :].bitcast(I32),
             scales[0, SCALE_ROWS * q : SCALE_ROWS * (q + 1), :].bitcast(I32),
@@ -45,12 +45,12 @@ def tile_list_weighedpicks_solo_store_plain_kernel(
         second_list = sbuf.tile([P, O // 16], U16, name="second_list")
         entry_list = sbuf.tile([P, N // 16], U16, name="entry_list")
 
-        xt_all = sbuf.tile([P, T], U32, name="xt_all", align_bytes=64)
-        xt_plane = sbuf.tile([P, T], U8, name="xt_plane", align_bytes=64)
+        xt_all = sbuf.tile([P, T], U32, name="xt_all", tag="tokens_then_scales", align_bytes=64)
+        xt_plane = sbuf.tile([P, T], U8, name="xt_plane", tag="codes", align_bytes=64)
         w_all = sbuf.tile([P, R], U16, name="w_all", align_bytes=64)
         w_plane = sbuf.tile([P, R], U8, name="w_plane", align_bytes=64)
         vs_all = sbuf.tile([P, S], U16, name="vs_all", align_bytes=64)
-        vs_plane = sbuf.tile([P, S], U8, name="vs_plane", align_bytes=64)
+        vs_plane = sbuf.tile([P, S], U8, name="vs_plane", tag="plane_then_hid", align_bytes=64)
         first_weight = sbuf.tile([P, PACK], F32, name="first_weight")
         second_weight = sbuf.tile([P, PACK], F32, name="second_weight")
 
@@ -58,74 +58,105 @@ def tile_list_weighedpicks_solo_store_plain_kernel(
             nc.vector.memset(plane[:].bitcast(I32), 0)
 
         nc.sync.dma_start(token_list[:], offs)
+        w_rows = sbuf.tile([SCALE_ROWS, QUADRANTS, R // 4], I32, name="w_rows")
+        nc.sync.dma_start(w_rows[:], w_scales[0].bitcast(I32).rearrange("(q r) c -> r q c", r=SCALE_ROWS))
         nc.sync.dma_start(xt_all[:].bitcast(I32), xt_words[0].rearrange("p c b -> p (c b)").bitcast(I32))
-        nc.scalar.dma_start(w_all[:].bitcast(I32), w_words[0].bitcast(I32))
-        load_scale_rows(nc.sync, xt_plane, xt_scales)
-        load_scale_rows(nc.sync, w_plane, w_scales)
-        nc.gpsimd.dma_start(first_weight[:], sa.rearrange("(p t) o -> p (t o)", t=PACK))
-        nc.gpsimd.dma_start(second_weight[:], sb.rearrange("(p t) o -> p (t o)", t=PACK))
+        load_scale_rows(nc.scalar, xt_plane, xt_scales, (0, 1))
+        load_scale_rows(nc.sync, xt_plane, xt_scales, (2, 3))
+        nc.sync.dma_start(w_all[:].bitcast(I32), w_words[0].bitcast(I32))
         nc.sync.dma_start(first_list[:], offs2)
         nc.sync.dma_start(second_list[:], offs3)
+        nc.sync.dma_start(first_weight[:], sa.rearrange("(p t) o -> p (t o)", t=PACK))
+        nc.sync.dma_start(second_weight[:], sb.rearrange("(p t) o -> p (t o)", t=PACK))
         nc.sync.dma_start(entry_list[:], offs4)
         nc.sync.dma_start(vs_all[:].bitcast(I32), vs_words[0].bitcast(I32))
-        load_scale_rows(nc.sync, vs_plane, vs_scales)
+        load_scale_rows(nc.sync, vs_plane, vs_scales, range(QUADRANTS))
 
-        x_codes = sbuf.tile([P, J], U32, name="x_codes", align_bytes=64)
-        x_scale = sbuf.tile([P, J], U8, name="x_scale", align_bytes=64)
+        for q in range(QUADRANTS):
+            nc.vector.tensor_copy(w_plane[QUADRANT * q : QUADRANT * q + SCALE_ROWS, :].bitcast(I32), w_rows[:, q, :])
+
+        w_columns = w_plane[:].rearrange("p (m t) -> p t m", t=PACK)
+        w_scale_first = sbuf.tile([P, P], U8, name="w_scale_first", align_bytes=64)
+        nc.vector.tensor_copy(w_scale_first[:], w_columns[:, 0, :])
+
+        x_codes = sbuf.tile([P, J], U32, name="x_codes", tag="codes", align_bytes=64)
+        x_scale = sbuf.tile([P, J], U8, name="x_scale", tag="scale", align_bytes=64)
         nc.vector.tensor_copy(x_scale[:], xt_plane[:].indirect(token_list[:]))
-        nc.vector.tensor_copy(x_codes[:], xt_all[:].indirect(token_list[:]))
+        slot_halves = [slice(0, J // 2), slice(J // 2, J)]
+        for slots in slot_halves:
+            nc.vector.tensor_copy(
+                x_codes[:, slots], xt_all[:].indirect(token_list[:, slots.start // 16 : slots.stop // 16])
+            )
 
-        w_scale = sbuf.tile([P, PACK, P], U8, name="w_scale", align_bytes=64)
-        nc.vector.tensor_copy(w_scale[:], w_plane[:].rearrange("p (m t) -> p t m", t=PACK))
+        w_scale_rest = sbuf.tile(
+            [P, PACK - 1, P], U8, name="w_scale_rest", tag="tokens_then_scales", align_bytes=64
+        )
+        nc.vector.tensor_copy(w_scale_rest[:], w_columns[:, 1:, :])
+        w_scale = [w_scale_first[:]] + [w_scale_rest[:, i, :] for i in range(PACK - 1)]
         w_codes = [sbuf.tile([P, P], U16, name=f"w_codes{t}", align_bytes=64) for t in range(PACK)]
         for t in range(PACK):
             nc.scalar.copy(w_codes[t][:], w_all[:, t::PACK])
 
-        hidden = []
-        for t in range(PACK):
-            sums = psum.tile([P, J], F32, name=f"sums{t}")
+        hidden = [sbuf.tile([P, J], F32, name=f"hidden{t}") for t in range(PACK)]
+        pieces = [(0, slot_halves[0], nc.scalar.copy), (0, slot_halves[1], nc.vector.tensor_copy)]
+        pieces += [(t, slice(0, J), nc.vector.tensor_copy) for t in range(1, PACK)]
+        for t, slots, copy_out in pieces:
+            sums = psum.tile([P, slots.stop - slots.start], F32, name=f"sums{t}_{slots.start}")
             nc.tensor.matmul_mx(
                 out=sums[:],
                 lhsT=w_codes[t][:].bitcast(E2M1X4),
-                lhsT_scale=w_scale[:, t, :],
-                rhs=x_codes[:].bitcast(E5M2X4),
-                rhs_scale=x_scale[:],
+                lhsT_scale=w_scale[t],
+                rhs=x_codes[:, slots].bitcast(E5M2X4),
+                rhs_scale=x_scale[:, slots],
                 start=True,
                 stop=True,
             )
-            rows = sbuf.tile([P, J], F32, name=f"hidden{t}")
-            nc.vector.tensor_copy(rows[:], sums[:])
-            hidden.append(rows)
+            copy_out(hidden[t][:, slots], sums[:])
 
-        v_codes = sbuf.tile([P, N], U16, name="v_codes", align_bytes=64)
-        v_scale = sbuf.tile([P, N], U8, name="v_scale", align_bytes=64)
+        v_codes = sbuf.tile([P, N], U16, name="v_codes", tag="codes", align_bytes=64)
+        v_scale = sbuf.tile([P, N], U8, name="v_scale", tag="scale", align_bytes=64)
         nc.vector.tensor_copy(v_codes[:], vs_all[:].indirect(entry_list[:]))
         nc.vector.tensor_copy(v_scale[:], vs_plane[:].indirect(entry_list[:]))
 
-        hid = sbuf.tile([P, O, PACK], BF16, name="hid", align_bytes=64)
-        for pair in range(PACK // 2):
-            first = sbuf.tile([P, 2, O], F32, name=f"first{pair}")
-            second = sbuf.tile([P, 2, O], F32, name=f"second{pair}")
-            for i in range(2):
-                t = 2 * pair + i
-                nc.scalar.activation(
-                    first[:, i, :], hidden[t][:].indirect(first_list[:]), COPY, scale=first_weight[:, t : t + 1]
-                )
-                nc.scalar.activation(
-                    second[:, i, :], hidden[t][:].indirect(second_list[:]), COPY, scale=second_weight[:, t : t + 1]
-                )
+        hid = sbuf.tile([P, O, PACK], BF16, name="hid", tag="plane_then_hid", align_bytes=64)
+        hid_codes = sbuf.tile([P, O], U32, name="hid_codes", align_bytes=64)
+        hid_scale = sbuf.tile([P, O], U8, name="hid_scale", align_bytes=64)
+        all_places = slice(0, O)
+        place_halves = [slice(0, O // 2), slice(O // 2, O)]
+
+        def fetch(products, t, place_list, weight, places):
+            nc.scalar.activation(
+                products[:, t % 2, places],
+                hidden[t][:].indirect(place_list[:, places.start // 16 : places.stop // 16]),
+                COPY,
+                scale=weight[:, t : t + 1],
+            )
+
+        def keep_larger(pair, places):
             nc.vector.tensor_tensor(
-                hid[:, :, 2 * pair : 2 * pair + 2],
-                first[:].rearrange("p i o -> p o i"),
-                second[:].rearrange("p i o -> p o i"),
+                hid[:, places, 2 * pair : 2 * pair + 2],
+                first[pair][:, :, places].rearrange("p i o -> p o i"),
+                second[pair][:, :, places].rearrange("p i o -> p o i"),
                 MAX,
             )
 
-        hid_codes = sbuf.tile([P, O], U32, name="hid_codes", align_bytes=64)
-        hid_scale = sbuf.tile([P, O], U8, name="hid_scale", align_bytes=64)
-        nc.vector.quantize_mx(
-            out=hid_codes[:].bitcast(E4M3X4), scales=hid_scale[:], in_=hid[:].rearrange("p o t -> p (o t)")
-        )
+        first = [sbuf.tile([P, 2, O], F32, name=f"first{pair}") for pair in range(2)]
+        second = [sbuf.tile([P, 2, O], F32, name=f"second{pair}") for pair in range(2)]
+        for t in range(PACK):
+            fetch(first[t // 2], t, first_list, first_weight, all_places)
+            if t < PACK - 1:
+                fetch(second[t // 2], t, second_list, second_weight, all_places)
+            if t == 1:
+                keep_larger(0, all_places)
+        for places in place_halves:
+            fetch(second[1], PACK - 1, second_list, second_weight, places)
+            keep_larger(1, places)
+        for places in place_halves:
+            nc.vector.quantize_mx(
+                out=hid_codes[:, places].bitcast(E4M3X4),
+                scales=hid_scale[:, places],
+                in_=hid[:, places, :].rearrange("p o t -> p (o t)"),
+            )
 
         for half, (copy_out, queue) in enumerate(((nc.vector.tensor_copy, nc.sync), (nc.scalar.copy, nc.scalar))):
             cols = slice(P * half, P * (half + 1))

@@ -45,8 +45,8 @@ def tile_list_weighedpicks_solo_store_plain_kernel(
         second_list = sbuf.tile([P, O // 16], U16, name="second_list")
         entry_list = sbuf.tile([P, N // 16], U16, name="entry_list")
 
-        xt_all = sbuf.tile([P, T], U32, name="xt_all", tag="tokens_then_scales", align_bytes=64)
-        xt_plane = sbuf.tile([P, T], U8, name="xt_plane", tag="codes", align_bytes=64)
+        xt_all = sbuf.tile([P, T], U32, name="xt_all", align_bytes=64)
+        xt_plane = sbuf.tile([P, T], U8, name="xt_plane", tag="tokens_then_scales", align_bytes=64)
         w_all = sbuf.tile([P, R], U16, name="w_all", align_bytes=64)
         w_plane = sbuf.tile([P, R], U8, name="w_plane", align_bytes=64)
         vs_all = sbuf.tile([P, S], U16, name="vs_all", align_bytes=64)
@@ -57,20 +57,20 @@ def tile_list_weighedpicks_solo_store_plain_kernel(
         for plane in (xt_plane, w_plane, vs_plane):
             nc.vector.memset(plane[:].bitcast(I32), 0)
 
-        nc.sync.dma_start(token_list[:], offs)
         w_rows = sbuf.tile([SCALE_ROWS, QUADRANTS, R // 4], I32, name="w_rows")
         nc.sync.dma_start(w_rows[:], w_scales[0].bitcast(I32).rearrange("(q r) c -> r q c", r=SCALE_ROWS))
+        nc.sync.dma_start(token_list[:], offs)
         nc.sync.dma_start(xt_all[:].bitcast(I32), xt_words[0].rearrange("p c b -> p (c b)").bitcast(I32))
         load_scale_rows(nc.scalar, xt_plane, xt_scales, (0, 1))
         load_scale_rows(nc.sync, xt_plane, xt_scales, (2, 3))
         nc.sync.dma_start(w_all[:].bitcast(I32), w_words[0].bitcast(I32))
         nc.sync.dma_start(first_list[:], offs2)
-        nc.sync.dma_start(second_list[:], offs3)
         nc.sync.dma_start(first_weight[:], sa.rearrange("(p t) o -> p (t o)", t=PACK))
+        nc.sync.dma_start(second_list[:], offs3)
         nc.sync.dma_start(second_weight[:], sb.rearrange("(p t) o -> p (t o)", t=PACK))
         nc.sync.dma_start(entry_list[:], offs4)
-        nc.sync.dma_start(vs_all[:].bitcast(I32), vs_words[0].bitcast(I32))
         load_scale_rows(nc.sync, vs_plane, vs_scales, range(QUADRANTS))
+        nc.sync.dma_start(vs_all[:].bitcast(I32), vs_words[0].bitcast(I32))
 
         for q in range(QUADRANTS):
             nc.vector.tensor_copy(w_plane[QUADRANT * q : QUADRANT * q + SCALE_ROWS, :].bitcast(I32), w_rows[:, q, :])
@@ -81,12 +81,12 @@ def tile_list_weighedpicks_solo_store_plain_kernel(
 
         x_codes = sbuf.tile([P, J], U32, name="x_codes", tag="codes", align_bytes=64)
         x_scale = sbuf.tile([P, J], U8, name="x_scale", tag="scale", align_bytes=64)
-        nc.vector.tensor_copy(x_scale[:], xt_plane[:].indirect(token_list[:]))
         slot_halves = [slice(0, J // 2), slice(J // 2, J)]
-        for slots in slot_halves:
-            nc.vector.tensor_copy(
-                x_codes[:, slots], xt_all[:].indirect(token_list[:, slots.start // 16 : slots.stop // 16])
-            )
+        for picked, window in ((x_codes, xt_all), (x_scale, xt_plane)):
+            for slots in slot_halves:
+                nc.vector.tensor_copy(
+                    picked[:, slots], window[:].indirect(token_list[:, slots.start // 16 : slots.stop // 16])
+                )
 
         w_scale_rest = sbuf.tile(
             [P, PACK - 1, P], U8, name="w_scale_rest", tag="tokens_then_scales", align_bytes=64
@@ -115,8 +115,8 @@ def tile_list_weighedpicks_solo_store_plain_kernel(
 
         v_codes = sbuf.tile([P, N], U16, name="v_codes", tag="codes", align_bytes=64)
         v_scale = sbuf.tile([P, N], U8, name="v_scale", tag="scale", align_bytes=64)
-        nc.vector.tensor_copy(v_codes[:], vs_all[:].indirect(entry_list[:]))
         nc.vector.tensor_copy(v_scale[:], vs_plane[:].indirect(entry_list[:]))
+        nc.vector.tensor_copy(v_codes[:], vs_all[:].indirect(entry_list[:]))
 
         hid = sbuf.tile([P, O, PACK], BF16, name="hid", tag="plane_then_hid", align_bytes=64)
         hid_codes = sbuf.tile([P, O], U32, name="hid_codes", align_bytes=64)

@@ -22,6 +22,7 @@ PACK = 4
 QUADRANTS = 4
 QUADRANT = 32
 SCALE_ROWS = 4
+HALF = 64
 
 
 def load_scale_rows(queue, plane, scales, quadrants):
@@ -48,21 +49,21 @@ def tile_list_weighedpicks_solo_store_plain_kernel(
         xt_all = sbuf.tile([P, T], U32, name="xt_all", align_bytes=64)
         xt_plane = sbuf.tile([P, T], U8, name="xt_plane", tag="tokens_then_scales", align_bytes=64)
         w_all = sbuf.tile([P, R], U16, name="w_all", align_bytes=64)
-        w_plane = sbuf.tile([P, R], U8, name="w_plane", align_bytes=64)
+        w_plane = sbuf.tile([P, 2, R], U8, name="w_plane", align_bytes=64)
         vs_all = sbuf.tile([P, S], U16, name="vs_all", align_bytes=64)
         vs_plane = sbuf.tile([P, S], U8, name="vs_plane", tag="plane_then_hid", align_bytes=64)
         first_weight = sbuf.tile([P, PACK], F32, name="first_weight")
         second_weight = sbuf.tile([P, PACK], F32, name="second_weight")
 
-        for plane in (xt_plane, w_plane, vs_plane):
-            nc.vector.memset(plane[:].bitcast(I32), 0)
+        nc.vector.memset(xt_plane[:].bitcast(I32), 0)
+        nc.vector.memset(w_plane[:HALF].rearrange("p h c -> p (h c)").bitcast(I32), 0)
+        nc.vector.memset(vs_plane[:].bitcast(I32), 0)
 
         w_rows = sbuf.tile([SCALE_ROWS, QUADRANTS, R // 4], I32, name="w_rows")
-        nc.sync.dma_start(w_rows[:], w_scales[0].bitcast(I32).rearrange("(q r) c -> r q c", r=SCALE_ROWS))
+        nc.scalar.dma_start(w_rows[:], w_scales[0].bitcast(I32).rearrange("(q r) c -> r q c", r=SCALE_ROWS))
         nc.sync.dma_start(token_list[:], offs)
         nc.sync.dma_start(xt_all[:].bitcast(I32), xt_words[0].rearrange("p c b -> p (c b)").bitcast(I32))
-        load_scale_rows(nc.scalar, xt_plane, xt_scales, (0, 1))
-        load_scale_rows(nc.sync, xt_plane, xt_scales, (2, 3))
+        load_scale_rows(nc.sync, xt_plane, xt_scales, range(QUADRANTS))
         nc.sync.dma_start(w_all[:].bitcast(I32), w_words[0].bitcast(I32))
         nc.sync.dma_start(first_list[:], offs2)
         nc.sync.dma_start(first_weight[:], sa.rearrange("(p t) o -> p (t o)", t=PACK))
@@ -72,26 +73,28 @@ def tile_list_weighedpicks_solo_store_plain_kernel(
         load_scale_rows(nc.sync, vs_plane, vs_scales, range(QUADRANTS))
         nc.sync.dma_start(vs_all[:].bitcast(I32), vs_words[0].bitcast(I32))
 
-        for q in range(QUADRANTS):
-            nc.vector.tensor_copy(w_plane[QUADRANT * q : QUADRANT * q + SCALE_ROWS, :].bitcast(I32), w_rows[:, q, :])
+        for q in range(2):
+            nc.vector.tensor_copy(w_plane[QUADRANT * q : QUADRANT * q + SCALE_ROWS].bitcast(I32), w_rows[:, q::2, :])
+        nc.vector.tensor_copy(w_plane[HALF:, 0, :].bitcast(I32), w_plane[:HALF, 1, :].bitcast(I32))
 
-        w_columns = w_plane[:].rearrange("p (m t) -> p t m", t=PACK)
+        w_columns = w_plane[:, 0, :].rearrange("p (m t) -> p t m", t=PACK)
         w_scale_first = sbuf.tile([P, P], U8, name="w_scale_first", align_bytes=64)
         nc.vector.tensor_copy(w_scale_first[:], w_columns[:, 0, :])
 
         x_codes = sbuf.tile([P, J], U32, name="x_codes", tag="codes", align_bytes=64)
         x_scale = sbuf.tile([P, J], U8, name="x_scale", tag="scale", align_bytes=64)
         slot_halves = [slice(0, J // 2), slice(J // 2, J)]
-        for picked, window in ((x_codes, xt_all), (x_scale, xt_plane)):
-            for slots in slot_halves:
-                nc.vector.tensor_copy(
-                    picked[:, slots], window[:].indirect(token_list[:, slots.start // 16 : slots.stop // 16])
-                )
+        nc.vector.tensor_copy(x_codes[:], xt_all[:].indirect(token_list[:]))
+        for slots in slot_halves:
+            nc.vector.tensor_copy(
+                x_scale[:, slots], xt_plane[:].indirect(token_list[:, slots.start // 16 : slots.stop // 16])
+            )
 
         w_scale_rest = sbuf.tile(
             [P, PACK - 1, P], U8, name="w_scale_rest", tag="tokens_then_scales", align_bytes=64
         )
-        nc.vector.tensor_copy(w_scale_rest[:], w_columns[:, 1:, :])
+        for t in range(1, PACK):
+            nc.gpsimd.tensor_copy(w_scale_rest[:, t - 1, :], w_columns[:, t, :])
         w_scale = [w_scale_first[:]] + [w_scale_rest[:, i, :] for i in range(PACK - 1)]
         w_codes = [sbuf.tile([P, P], U16, name=f"w_codes{t}", align_bytes=64) for t in range(PACK)]
         for t in range(PACK):

from contextlib import ExitStack

import concourse.mybir as mybir

K, T, J, R, O, N, S = 512, 1024, 256, 512, 128, 256, 1024
FLOPS = 2 * K * R * J + 2 * R * N * O

F32 = mybir.dt.float32
BF16 = mybir.dt.bfloat16
I32 = mybir.dt.int32
U32 = mybir.dt.uint32
U16 = mybir.dt.uint16
U8 = mybir.dt.uint8
E5M2X4 = mybir.dt.float8_e5m2_x4
E4M3X4 = mybir.dt.float8_e4m3fn_x4
E2M1X4 = mybir.dt.float4_e2m1fn_x4
COPY = mybir.ActivationFunctionType.Copy
MAX = mybir.AluOpType.max

P = 128
PACK = 4
QUADRANTS = 4
QUADRANT = 32
SCALE_ROWS = 4
HALF = 64


def load_scale_rows(queue, plane, scales, quadrants):
    for q in quadrants:
        queue.dma_start(
            plane[QUADRANT * q : QUADRANT * q + SCALE_ROWS, :].bitcast(I32),
            scales[0, SCALE_ROWS * q : SCALE_ROWS * (q + 1), :].bitcast(I32),
        )


def tile_list_weighedpicks_solo_store_plain_kernel(
    tc, xt_words, xt_scales, w_words, w_scales, sa, sb, vs_words, vs_scales, offs, offs2, offs3, offs4, out
):
    nc = tc.nc
    with ExitStack() as ctx:
        sbuf = ctx.enter_context(tc.tile_pool(name="sbuf", bufs=1))
        psum = ctx.enter_context(tc.psum_pool(name="psum", bufs=1))

        token_list = sbuf.tile([P, J // 16], U16, name="token_list")
        first_list = sbuf.tile([P, O // 16], U16, name="first_list")
        second_list = sbuf.tile([P, O // 16], U16, name="second_list")
        entry_list = sbuf.tile([P, N // 16], U16, name="entry_list")

        xt_all = sbuf.tile([P, T], U32, name="xt_all", align_bytes=64)
        xt_plane = sbuf.tile([P, T], U8, name="xt_plane", tag="tokens_then_scales", align_bytes=64)
        w_all = sbuf.tile([P, R], U16, name="w_all", align_bytes=64)
        w_plane = sbuf.tile([P, 2, R], U8, name="w_plane", align_bytes=64)
        vs_all = sbuf.tile([P, S], U16, name="vs_all", align_bytes=64)
        vs_plane = sbuf.tile([P, S], U8, name="vs_plane", tag="plane_then_hid", align_bytes=64)
        first_weight = sbuf.tile([P, PACK], F32, name="first_weight")
        second_weight = sbuf.tile([P, PACK], F32, name="second_weight")

        nc.vector.memset(xt_plane[:].bitcast(I32), 0)
        nc.vector.memset(w_plane[:HALF].rearrange("p h c -> p (h c)").bitcast(I32), 0)
        nc.vector.memset(vs_plane[:].bitcast(I32), 0)

        w_rows = sbuf.tile([SCALE_ROWS, QUADRANTS, R // 4], I32, name="w_rows")
        nc.scalar.dma_start(w_rows[:], w_scales[0].bitcast(I32).rearrange("(q r) c -> r q c", r=SCALE_ROWS))
        nc.sync.dma_start(token_list[:], offs)
        nc.sync.dma_start(xt_all[:].bitcast(I32), xt_words[0].rearrange("p c b -> p (c b)").bitcast(I32))
        load_scale_rows(nc.sync, xt_plane, xt_scales, range(QUADRANTS))
        nc.sync.dma_start(w_all[:].bitcast(I32), w_words[0].bitcast(I32))
        nc.sync.dma_start(first_list[:], offs2)
        nc.sync.dma_start(first_weight[:], sa.rearrange("(p t) o -> p (t o)", t=PACK))
        nc.sync.dma_start(second_list[:], offs3)
        nc.sync.dma_start(second_weight[:], sb.rearrange("(p t) o -> p (t o)", t=PACK))
        nc.sync.dma_start(entry_list[:], offs4)
        load_scale_rows(nc.sync, vs_plane, vs_scales, range(QUADRANTS))
        nc.sync.dma_start(vs_all[:].bitcast(I32), vs_words[0].bitcast(I32))

        for q in range(2):
            nc.vector.tensor_copy(w_plane[QUADRANT * q : QUADRANT * q + SCALE_ROWS].bitcast(I32), w_rows[:, q::2, :])
        nc.vector.tensor_copy(w_plane[HALF:, 0, :].bitcast(I32), w_plane[:HALF, 1, :].bitcast(I32))

        w_columns = w_plane[:, 0, :].rearrange("p (m t) -> p t m", t=PACK)
        w_scale_first = sbuf.tile([P, P], U8, name="w_scale_first", align_bytes=64)
        nc.vector.tensor_copy(w_scale_first[:], w_columns[:, 0, :])

        x_codes = sbuf.tile([P, J], U32, name="x_codes", tag="codes", align_bytes=64)
        x_scale = sbuf.tile([P, J], U8, name="x_scale", tag="scale", align_bytes=64)
        slot_halves = [slice(0, J // 2), slice(J // 2, J)]
        nc.vector.tensor_copy(x_codes[:], xt_all[:].indirect(token_list[:]))
        for slots in slot_halves:
            nc.vector.tensor_copy(
                x_scale[:, slots], xt_plane[:].indirect(token_list[:, slots.start // 16 : slots.stop // 16])
            )

        w_scale_rest = sbuf.tile(
            [P, PACK - 1, P], U8, name="w_scale_rest", tag="tokens_then_scales", align_bytes=64
        )
        for t in range(1, PACK):
            nc.gpsimd.tensor_copy(w_scale_rest[:, t - 1, :], w_columns[:, t, :])
        w_scale = [w_scale_first[:]] + [w_scale_rest[:, i, :] for i in range(PACK - 1)]
        w_codes = [sbuf.tile([P, P], U16, name=f"w_codes{t}", align_bytes=64) for t in range(PACK)]
        for t in range(PACK):
            nc.scalar.copy(w_codes[t][:], w_all[:, t::PACK])

        hidden = [sbuf.tile([P, J], F32, name=f"hidden{t}") for t in range(PACK)]
        pieces = [(0, slot_halves[0], nc.scalar.copy), (0, slot_halves[1], nc.vector.tensor_copy)]
        pieces += [(t, slice(0, J), nc.vector.tensor_copy) for t in range(1, PACK)]
        for t, slots, copy_out in pieces:
            sums = psum.tile([P, slots.stop - slots.start], F32, name=f"sums{t}_{slots.start}")
            nc.tensor.matmul_mx(
                out=sums[:],
                lhsT=w_codes[t][:].bitcast(E2M1X4),
                lhsT_scale=w_scale[t],
                rhs=x_codes[:, slots].bitcast(E5M2X4),
                rhs_scale=x_scale[:, slots],
                start=True,
                stop=True,
            )
            copy_out(hidden[t][:, slots], sums[:])

        v_codes = sbuf.tile([P, N], U16, name="v_codes", tag="codes", align_bytes=64)
        v_scale = sbuf.tile([P, N], U8, name="v_scale", tag="scale", align_bytes=64)
        nc.vector.tensor_copy(v_scale[:], vs_plane[:].indirect(entry_list[:]))
        nc.vector.tensor_copy(v_codes[:], vs_all[:].indirect(entry_list[:]))

        hid = sbuf.tile([P, O, PACK], BF16, name="hid", tag="plane_then_hid", align_bytes=64)
        hid_codes = sbuf.tile([P, O], U32, name="hid_codes", align_bytes=64)
        hid_scale = sbuf.tile([P, O], U8, name="hid_scale", align_bytes=64)
        all_places = slice(0, O)
        place_halves = [slice(0, O // 2), slice(O // 2, O)]

        def fetch(products, t, place_list, weight, places):
            nc.scalar.activation(
                products[:, t % 2, places],
                hidden[t][:].indirect(place_list[:, places.start // 16 : places.stop // 16]),
                COPY,
                scale=weight[:, t : t + 1],
            )

        def keep_larger(pair, places):
            nc.vector.tensor_tensor(
                hid[:, places, 2 * pair : 2 * pair + 2],
                first[pair][:, :, places].rearrange("p i o -> p o i"),
                second[pair][:, :, places].rearrange("p i o -> p o i"),
                MAX,
            )

        first = [sbuf.tile([P, 2, O], F32, name=f"first{pair}") for pair in range(2)]
        second = [sbuf.tile([P, 2, O], F32, name=f"second{pair}") for pair in range(2)]
        for t in range(PACK):
            fetch(first[t // 2], t, first_list, first_weight, all_places)
            if t < PACK - 1:
                fetch(second[t // 2], t, second_list, second_weight, all_places)
            if t == 1:
                keep_larger(0, all_places)
        for places in place_halves:
            fetch(second[1], PACK - 1, second_list, second_weight, places)
            keep_larger(1, places)
        for places in place_halves:
            nc.vector.quantize_mx(
                out=hid_codes[:, places].bitcast(E4M3X4),
                scales=hid_scale[:, places],
                in_=hid[:, places, :].rearrange("p o t -> p (o t)"),
            )

        for half, (copy_out, queue) in enumerate(((nc.vector.tensor_copy, nc.sync), (nc.scalar.copy, nc.scalar))):
            cols = slice(P * half, P * (half + 1))
            product = psum.tile([P, O], F32, name=f"product{half}")
            nc.tensor.matmul_mx(
                out=product[:],
                lhsT=v_codes[:, cols].bitcast(E2M1X4),
                lhsT_scale=v_scale[:, cols],
                rhs=hid_codes[:].bitcast(E4M3X4),
                rhs_scale=hid_scale[:],
                start=True,
                stop=True,
            )
            result = sbuf.tile([P, O], F32, name=f"result{half}")
            copy_out(result[:], product[:])
            queue.dma_start(out[cols, :], result[:])
